import numpy as np
import ml_dtypes


def mxq(x, axis, fmt="e4m3"):
    dtype, down = {"e4m3": (ml_dtypes.float8_e4m3fn, 7), "e5m2": (ml_dtypes.float8_e5m2, 14)}[fmt]
    v = np.moveaxis(np.asarray(x, np.float32).astype(ml_dtypes.bfloat16).astype(np.float64), axis, -1)
    blocks = v.reshape(v.shape[:-1] + (-1, 32))
    amax = np.abs(blocks).max(-1, keepdims=True)
    byte = np.maximum(np.where(amax > 0, np.frexp(amax)[1] - 1 + 127, 0) - down, 1)
    scale = np.exp2(byte - 127.0)
    codes = (blocks / scale).astype(np.float32).astype(dtype).astype(np.float64)
    return np.moveaxis((codes * scale).reshape(v.shape), -1, axis)


WIDE = False


def mx_kscale(k):
    if not WIDE:
        return np.ones(k)
    levels = np.array([10, -10, 5, -5, 0])
    if k % 512:
        return np.exp2(np.random.permutation(np.resize(levels, k // 32))).repeat(32)
    a = np.empty((k // 512, 16))
    for p in range(k // 512):
        a[p, :8] = np.random.permutation(np.resize(levels, 8))
        for g in range(8):
            far = levels[np.abs(levels - a[p, g]) >= 10]
            a[p, g + 8] = far[np.random.randint(len(far))]
    return np.exp2(a.ravel()).repeat(32)


def f64(x):
    return np.asarray(x).astype(np.float64)


def striped8(idx):
    return np.asarray(idx).reshape(8, -1, 16).transpose(0, 2, 1).reshape(128, -1).astype(np.uint16)


def unstriped8(offs):
    return offs.reshape(8, 16, -1).transpose(0, 2, 1).reshape(8, -1).astype(np.int64)


def pick8(x, idx, run):
    r = np.arange(len(x))
    return x[r[:, None], idx[r % (8 * run) // run]]


E2M1 = np.array([0.0, 0.5, 1.0, 1.5, 2.0, 3.0, 4.0, 6.0, -0.0, -0.5, -1.0, -1.5, -2.0, -3.0, -4.0, -6.0])


def pack_weight(w, fmt):
    k, n = w.shape
    w = f64(np.asarray(w, np.float32).astype(ml_dtypes.bfloat16)).reshape(k // 32, 32, n)
    amax = np.abs(w).max(1)
    if fmt == "e4m3":
        byte = np.frexp(amax)[1] - 1 + 127 - 7
    else:
        mant, ex = np.frexp(amax / 6.0)
        byte = np.where(mant > 0.5, ex, ex - 1) + 127
    byte = np.clip(np.where(amax > 0, byte, 1), 1, 254)
    scaled = (w * np.exp2(127.0 - byte)[:, None, :]).reshape(k, n).astype(np.float32)
    by_word = np.ascontiguousarray(scaled.reshape(k // 512, 128, 4, n).transpose(0, 1, 3, 2))
    if fmt == "e4m3":
        words = by_word.astype(ml_dtypes.float8_e4m3fn).view(np.uint8)
    else:
        c = by_word.astype(ml_dtypes.float4_e2m1fn).view(np.uint8) & 0xF
        words = (c[..., 0::2] | (c[..., 1::2] << 4)).reshape(k // 512, 128, 2 * n)
    return np.ascontiguousarray(words), np.ascontiguousarray(byte.astype(np.uint8).reshape(k // 512, 16, n))


def unpack_weight(words, scales, fmt):
    g, _, n = scales.shape
    words = np.ascontiguousarray(words).reshape(g, 128, n, -1)
    if fmt == "e4m3":
        vals = words.view(ml_dtypes.float8_e4m3fn).astype(np.float64)
    else:
        nib = np.empty((g, 128, n, 4), np.uint8)
        nib[..., 0::2] = words & 0xF
        nib[..., 1::2] = words >> 4
        vals = E2M1[nib]
    vals = vals * np.repeat(np.exp2(scales.astype(np.float64) - 127.0), 8, axis=1)[..., None]
    return vals.transpose(0, 1, 3, 2).reshape(g * 512, n)


D, T, I, Q, G = 512, 1024, 512, 128, 64


def setup_inputs():
    n = np.random.standard_normal
    idx = np.stack([np.random.permutation(T)[:I] for _ in range(8)])
    idx2 = np.stack([np.random.permutation(T)[:I] for _ in range(8)])
    idx3 = np.stack([np.random.permutation(T)[:I] for _ in range(8)])
    fd = mx_kscale(D)
    keysp = pack_weight(n((D, T)) / fd[:, None], "e4m3")
    return {
        "query": (n((D, Q)) * 1.2 / np.sqrt(D) * fd[:, None]).astype(np.float32),
        "keys_words": keysp[0],
        "keys_scales": keysp[1],
        "lam": (np.random.uniform(0.2, 0.7, (Q, 1))).astype(np.float32),
        "base": (0.3 * n((Q, I))).astype(np.float32),
        "gain2": (np.random.uniform(0.5, 2.0, (Q, 1))).astype(np.float32),
        "offs": striped8(idx),
        "offs2": striped8(idx2),
        "offs3": striped8(idx3),
    }


def reference(query, keys_words, keys_scales, lam, base, gain2, offs, offs2, offs3):
    idx = unstriped8(offs)
    idx2 = unstriped8(offs2)
    idx3 = unstriped8(offs3)
    keysu = unpack_weight(keys_words, keys_scales, "e4m3")
    queryq = mxq(f64(query), 0, "e4m3")
    a = queryq.T @ keysu
    mx3 = np.maximum(np.maximum(pick8(a, idx, 16), pick8(a, idx2, 16)), pick8(a, idx3, 16))
    mn3 = np.minimum(np.minimum(pick8(a, idx, 16), pick8(a, idx2, 16)), pick8(a, idx3, 16))
    s = (pick8(a, idx, 16) + pick8(a, idx2, 16) + pick8(a, idx3, 16)) / 3.0 - (mx3 - mn3) * f64(lam)
    bm = s.reshape(Q, G, I // G).max(axis=2)
    bmr = np.repeat(bm, I // G, axis=1)
    p = np.exp(s - bmr)
    pg = p.reshape(Q, G, I // G).sum(axis=2)
    eg = np.exp(bm - np.max(bm, axis=1, keepdims=True))
    k0 = eg / np.sum(eg, axis=1, keepdims=True) / pg
    kr = np.repeat(k0, I // G, axis=1)
    w = p * kr
    y = np.tanh(w * f64(gain2) * 128.0) + f64(base)
    return y

@@ -1,0 +1,178 @@
+from contextlib import ExitStack
+
+import concourse.mybir as mybir
+
+D, T, I, Q, G = 512, 1024, 512, 128, 64
+RUN = I // G
+FLOPS = 2 * D * T * Q
+
+F32 = mybir.dt.float32
+BF16 = mybir.dt.bfloat16
+I32 = mybir.dt.int32
+U32 = mybir.dt.uint32
+U16 = mybir.dt.uint16
+U8 = mybir.dt.uint8
+FP8X4 = mybir.dt.float8_e4m3fn_x4
+ALU = mybir.AluOpType
+ACT = mybir.ActivationFunctionType
+AX = mybir.AxisListType
+
+P = 128
+PACK = 4
+CHUNKS = 4
+CW = T // CHUNKS
+HALVES = 2
+HS = I // HALVES
+HG = G // HALVES
+BIG = 3.0e38
+
+
+def tile_attend_spreadof3_bestofruns_gated_heads_kernel(
+    tc, query, keys_words, keys_scales, lam, base, gain2, offs, offs2, offs3, out
+):
+    nc = tc.nc
+    with ExitStack() as ctx:
+        lists = ctx.enter_context(tc.tile_pool(name="lists", bufs=1))
+        sb = ctx.enter_context(tc.tile_pool(name="sb", bufs=1))
+        ps = ctx.enter_context(tc.psum_pool(name="ps", bufs=1))
+
+        q_raw = sb.tile([P, PACK, Q], F32, name="q_raw")
+        nc.sync.dma_start(out=q_raw[:], in_=query.rearrange("(p j) q -> p j q", j=PACK))
+
+        k_planes = sb.tile([P, CW], U8, name="k_planes", align_bytes=64)
+        nc.vector.memset(k_planes[:].bitcast(I32), 0)
+        scale_words = keys_scales[0].bitcast(I32)
+        for quad in range(4):
+            nc.scalar.dma_start(
+                out=k_planes[32 * quad : 32 * quad + 16, :].bitcast(I32),
+                in_=scale_words[4 * quad : 4 * quad + 4, :].rearrange("r (j c) -> j r c", j=CHUNKS),
+            )
+
+        word_rows = keys_words[0].rearrange("p n t -> p (n t)")
+        k_words = []
+        for u in range(2):
+            kw = sb.tile([P, T // 2], U32, name=f"k_words{u}", align_bytes=64)
+            nc.sync.dma_start(out=kw[:].bitcast(I32), in_=word_rows[:, u * 2 * T : (u + 1) * 2 * T].bitcast(I32))
+            k_words.append(kw)
+
+        o1 = lists.tile([P, I // 16], U16, name="o1")
+        o2 = lists.tile([P, I // 16], U16, name="o2")
+        o3 = lists.tile([P, I // 16], U16, name="o3")
+        nc.sync.dma_start(o2[:], offs2)
+        nc.sync.dma_start(o1[:], offs)
+        nc.sync.dma_start(o3[:], offs3)
+        lam_t = sb.tile([P, 1], F32, name="lam_t")
+        gain_t = sb.tile([P, 1], F32, name="gain_t")
+        base_t = sb.tile([P, I], F32, name="base_t")
+        nc.sync.dma_start(out=lam_t[:], in_=lam)
+        nc.sync.dma_start(out=gain_t[:], in_=gain2)
+        nc.sync.dma_start(out=base_t[:], in_=base)
+
+        q_bf = sb.tile([P, Q, PACK], BF16, name="q_bf", align_bytes=64)
+        nc.vector.tensor_copy(
+            out=q_bf[:].rearrange("p (c i) t -> p c t i", i=4),
+            in_=q_raw[:].rearrange("p t (c i) -> p c t i", i=4),
+        )
+        q_words = sb.tile([P, Q], U32, name="q_words", align_bytes=64)
+        q_plane = sb.tile([P, Q], U8, name="q_plane", align_bytes=64)
+        nc.vector.quantize_mx(
+            out=q_words[:].bitcast(FP8X4), scales=q_plane[:], in_=q_bf[:].rearrange("p q t -> p (q t)")
+        )
+
+        a = sb.tile([P, T], F32, name="a")
+        for j in range(CHUNKS):
+            bank = ps.tile([P, CW], F32, name=f"bank{j}")
+            kw = k_words[j // 2]
+            c0 = (j % 2) * CW
+            nc.tensor.matmul_mx(
+                out=bank[:],
+                lhsT=q_words[:].bitcast(FP8X4),
+                lhsT_scale=q_plane[:],
+                rhs=kw[:, c0 : c0 + CW].bitcast(FP8X4),
+                rhs_scale=k_planes[4 * j : P, :],
+                start=True,
+                stop=True,
+            )
+            if j % 2 == 0:
+                nc.vector.tensor_copy(out=a[:, j * CW : (j + 1) * CW], in_=bank[:])
+            else:
+                nc.scalar.activation(out=a[:, j * CW : (j + 1) * CW], in_=bank[:], func=ACT.Copy)
+
+        def halves(name, width=HS):
+            return [sb.tile([P, width], F32, name=f"{name}{h}") for h in range(HALVES)]
+
+        def cut(lst, h):
+            return a[:].indirect(lst[:, h * HS // 16 : (h + 1) * HS // 16])
+
+        g1, g2, g3 = halves("g1"), halves("g2"), halves("g3")
+        z, mid, c, mean = halves("z"), halves("mid"), halves("c"), halves("mean")
+        az, ac, mx, spread, ns = halves("az"), halves("ac"), halves("mx"), halves("spread"), halves("ns")
+        p, w, th, y = halves("p"), halves("w"), halves("th"), halves("y")
+        pg, rpg, k = halves("pg", HG), halves("rpg", HG), halves("k", HG)
+        nbm = sb.tile([P, G], F32, name="nbm")
+        eg = sb.tile([P, G], F32, name="eg")
+        shift = halves("shift", 1)
+        eg_sum = sb.tile([P, 1], F32, name="eg_sum")
+        r_sum = sb.tile([P, 1], F32, name="r_sum")
+        row_gain = sb.tile([P, 1], F32, name="row_gain")
+
+        def runs(t):
+            return t.rearrange("p (g e) -> p g e", e=RUN)
+
+        both = range(HALVES)
+        for h in both:
+            nc.vector.tensor_copy(out=g1[h][:], in_=cut(o1, h))
+            nc.scalar.activation(out=g2[h][:], in_=cut(o2, h), func=ACT.Copy)
+        for h in both:
+            nc.scalar.activation(out=g3[h][:], in_=cut(o3, h), func=ACT.Copy)
+        for h in both:
+            nc.vector.tensor_tensor(out=z[h][:], in0=g1[h][:], in1=g2[h][:], op=ALU.subtract)
+        for h in both:
+            nc.vector.scalar_tensor_tensor(
+                out=mid[h][:], in0=z[h][:], scalar=0.5, in1=g2[h][:], op0=ALU.mult, op1=ALU.add
+            )
+            nc.scalar.activation(out=az[h][:], in_=z[h][:], func=ACT.Abs, scale=0.5)
+        for h in both:
+            nc.vector.tensor_tensor(out=c[h][:], in0=g3[h][:], in1=mid[h][:], op=ALU.subtract)
+            nc.scalar.activation(out=ac[h][:], in_=c[h][:], func=ACT.Abs)
+        for h in both:
+            nc.vector.scalar_tensor_tensor(
+                out=mean[h][:], in0=c[h][:], scalar=1.0 / 3.0, in1=mid[h][:], op0=ALU.mult, op1=ALU.add
+            )
+        for h in both:
+            nc.vector.tensor_tensor(out=mx[h][:], in0=az[h][:], in1=ac[h][:], op=ALU.max)
+        for h in both:
+            nc.vector.tensor_tensor(out=spread[h][:], in0=mx[h][:], in1=az[h][:], op=ALU.add)
+        for h in both:
+            nc.vector.scalar_tensor_tensor(
+                out=ns[h][:], in0=spread[h][:], scalar=lam_t[:], in1=mean[h][:], op0=ALU.mult, op1=ALU.subtract
+            )
+        for h in both:
+            nc.vector.tensor_reduce(out=nbm[:, h * HG : (h + 1) * HG], in_=runs(ns[h][:]), axis=AX.X, op=ALU.min)
+        for h in both:
+            nc.vector.tensor_reduce(out=shift[h][:], in_=nbm[:, 0 : (h + 1) * HG], axis=AX.X, op=ALU.min)
+        for h in both:
+            nc.scalar.activation(out=p[h][:], in_=ns[h][:], func=ACT.Exp, scale=-1.0, bias=shift[h][:])
+        nc.scalar.activation(
+            out=eg[:], in_=nbm[:], func=ACT.Exp, scale=-1.0, bias=shift[HALVES - 1][:], accum_out=eg_sum[:]
+        )
+        for h in both:
+            nc.vector.tensor_reduce(out=pg[h][:], in_=runs(p[h][:]), axis=AX.X, op=ALU.add)
+        nc.vector.reciprocal(out=r_sum[:], in_=eg_sum[:])
+        for h in both:
+            nc.vector.reciprocal(out=rpg[h][:], in_=pg[h][:])
+        nc.vector.tensor_scalar(
+            out=row_gain[:], in0=r_sum[:], scalar1=gain_t[:], scalar2=128.0, op0=ALU.mult, op1=ALU.mult
+        )
+        for h in both:
+            nc.vector.scalar_tensor_tensor(
+                out=k[h][:], in0=rpg[h][:], scalar=BIG, in1=eg[:, h * HG : (h + 1) * HG], op0=ALU.min, op1=ALU.mult
+            )
+        for h in both:
+            nc.vector.tensor_tensor(
+                out=runs(w[h][:]), in0=runs(p[h][:]), in1=k[h][:].unsqueeze(2).to_broadcast([P, HG, RUN]), op=ALU.mult
+            )
+            nc.scalar.activation(out=th[h][:], in_=w[h][:], func=ACT.Tanh, scale=row_gain[:])
+        for h in both:
+            nc.vector.tensor_tensor(out=y[h][:], in0=th[h][:], in1=base_t[:, h * HS : (h + 1) * HS], op=ALU.add)
+            nc.sync.dma_start(out=out[:, h * HS : (h + 1) * HS], in_=y[h][:])

@@ -25,6 +25,8 @@ HALVES = 2
 HS = I // HALVES
 HG = G // HALVES
 BIG = 3.0e38
+QV = 22
+PASSES = ((0, 256), (256, 256), (512, 256), (768, 128), (896, 128))
 
 
 def tile_attend_spreadof3_bestofruns_gated_heads_kernel(
@@ -39,21 +41,24 @@ def tile_attend_spreadof3_bestofruns_gated_heads_kernel(
         q_raw = sb.tile([P, PACK, Q], F32, name="q_raw")
         nc.sync.dma_start(out=q_raw[:], in_=query.rearrange("(p j) q -> p j q", j=PACK))
 
+        word_rows = keys_words[0].rearrange("p n t -> p (n t)")
+        k_words = [sb.tile([P, T // 2], U32, name=f"k_words{u}", align_bytes=64) for u in range(2)]
+
+        def load_words(u):
+            nc.sync.dma_start(
+                out=k_words[u][:].bitcast(I32), in_=word_rows[:, u * 2 * T : (u + 1) * 2 * T].bitcast(I32)
+            )
+
+        load_words(0)
         k_planes = sb.tile([P, CW], U8, name="k_planes", align_bytes=64)
         nc.vector.memset(k_planes[:].bitcast(I32), 0)
         scale_words = keys_scales[0].bitcast(I32)
         for quad in range(4):
-            nc.scalar.dma_start(
+            nc.sync.dma_start(
                 out=k_planes[32 * quad : 32 * quad + 16, :].bitcast(I32),
                 in_=scale_words[4 * quad : 4 * quad + 4, :].rearrange("r (j c) -> j r c", j=CHUNKS),
             )
-
-        word_rows = keys_words[0].rearrange("p n t -> p (n t)")
-        k_words = []
-        for u in range(2):
-            kw = sb.tile([P, T // 2], U32, name=f"k_words{u}", align_bytes=64)
-            nc.sync.dma_start(out=kw[:].bitcast(I32), in_=word_rows[:, u * 2 * T : (u + 1) * 2 * T].bitcast(I32))
-            k_words.append(kw)
+        load_words(1)
 
         o1 = lists.tile([P, I // 16], U16, name="o1")
         o2 = lists.tile([P, I // 16], U16, name="o2")
@@ -69,10 +74,10 @@ def tile_attend_spreadof3_bestofruns_gated_heads_kernel(
         nc.sync.dma_start(out=base_t[:], in_=base)
 
         q_bf = sb.tile([P, Q, PACK], BF16, name="q_bf", align_bytes=64)
-        nc.vector.tensor_copy(
-            out=q_bf[:].rearrange("p (c i) t -> p c t i", i=4),
-            in_=q_raw[:].rearrange("p t (c i) -> p c t i", i=4),
-        )
+        q_dst = q_bf[:].rearrange("p (c i) t -> p c t i", i=4)
+        q_src = q_raw[:].rearrange("p t (c i) -> p c t i", i=4)
+        nc.vector.tensor_copy(out=q_dst[:, 0:QV], in_=q_src[:, 0:QV])
+        nc.scalar.copy(out=q_dst[:, QV : Q // 4], in_=q_src[:, QV : Q // 4])
         q_words = sb.tile([P, Q], U32, name="q_words", align_bytes=64)
         q_plane = sb.tile([P, Q], U8, name="q_plane", align_bytes=64)
         nc.vector.quantize_mx(
@@ -80,44 +85,95 @@ def tile_attend_spreadof3_bestofruns_gated_heads_kernel(
         )
 
         a = sb.tile([P, T], F32, name="a")
-        for j in range(CHUNKS):
-            bank = ps.tile([P, CW], F32, name=f"bank{j}")
-            kw = k_words[j // 2]
-            c0 = (j % 2) * CW
+        for n, (t0, width) in enumerate(PASSES):
+            bank = ps.tile([P, width], F32, name=f"bank{n}")
+            kw = k_words[t0 // (T // 2)]
+            c0 = t0 % (T // 2)
+            j, s0 = divmod(t0, CW)
             nc.tensor.matmul_mx(
                 out=bank[:],
                 lhsT=q_words[:].bitcast(FP8X4),
                 lhsT_scale=q_plane[:],
-                rhs=kw[:, c0 : c0 + CW].bitcast(FP8X4),
-                rhs_scale=k_planes[4 * j : P, :],
+                rhs=kw[:, c0 : c0 + width].bitcast(FP8X4),
+                rhs_scale=k_planes[4 * j : P, s0 : s0 + width],
                 start=True,
                 stop=True,
             )
-            if j % 2 == 0:
-                nc.vector.tensor_copy(out=a[:, j * CW : (j + 1) * CW], in_=bank[:])
+            if n % 2 == 1:
+                nc.vector.tensor_copy(out=a[:, t0 : t0 + width], in_=bank[:])
             else:
-                nc.scalar.activation(out=a[:, j * CW : (j + 1) * CW], in_=bank[:], func=ACT.Copy)
+                nc.scalar.activation(out=a[:, t0 : t0 + width], in_=bank[:], func=ACT.Copy)
 
         def halves(name, width=HS):
             return [sb.tile([P, width], F32, name=f"{name}{h}") for h in range(HALVES)]
 
-        def cut(lst, h):
-            return a[:].indirect(lst[:, h * HS // 16 : (h + 1) * HS // 16])
+        def half(t, h, width=HS):
+            return t[:, h * width : (h + 1) * width]
 
         g1, g2, g3 = halves("g1"), halves("g2"), halves("g3")
-        z, mid, c, mean = halves("z"), halves("mid"), halves("c"), halves("mean")
-        az, ac, mx, spread, ns = halves("az"), halves("ac"), halves("mx"), halves("spread"), halves("ns")
+        z, mid, c, u, v = halves("z"), halves("mid"), halves("c"), halves("u"), halves("v")
+        az, ac, mx, ns = halves("az"), halves("ac"), halves("mx"), halves("ns")
         p, w, th, y = halves("p"), halves("w"), halves("th"), halves("y")
-        pg, rpg, k = halves("pg", HG), halves("rpg", HG), halves("k", HG)
+        pg, rpg, k = halves("pg", HG + 1), halves("rpg", HG + 1), halves("k", HG)
         nbm = sb.tile([P, G], F32, name="nbm")
         eg = sb.tile([P, G], F32, name="eg")
         shift = halves("shift", 1)
-        eg_sum = sb.tile([P, 1], F32, name="eg_sum")
-        r_sum = sb.tile([P, 1], F32, name="r_sum")
+        gain128 = sb.tile([P, 1], F32, name="gain128")
         row_gain = sb.tile([P, 1], F32, name="row_gain")
 
         def runs(t):
             return t.rearrange("p (g e) -> p g e", e=RUN)
+
+        def tt(o, i0, i1, op):
+            nc.vector.tensor_tensor(out=o, in0=i0, in1=i1, op=op)
+
+        def stt(o, i0, s, i1, op0, op1):
+            nc.vector.scalar_tensor_tensor(out=o, in0=i0, scalar=s, in1=i1, op0=op0, op1=op1)
+
+        def f_u(h):
+            stt(u[h][:], az[h][:], lam_t[:], mid[h][:], ALU.mult, ALU.subtract)
+
+        def f_v(h):
+            stt(v[h][:], c[h][:], -1.0 / 3.0, u[h][:], ALU.mult, ALU.add)
+
+        def f_mx(h):
+            tt(mx[h][:], az[h][:], ac[h][:], ALU.max)
+
+        def f_ns(h):
+            stt(ns[h][:], mx[h][:], lam_t[:], v[h][:], ALU.mult, ALU.add)
+
+        def f_bm(h):
+            nc.vector.tensor_reduce(out=half(nbm, h, HG), in_=runs(ns[h][:]), axis=AX.X, op=ALU.min)
+
+        def f_shift(h):
+            nc.vector.tensor_reduce(out=shift[h][:], in_=nbm[:, 0 : (h + 1) * HG], axis=AX.X, op=ALU.min)
+
+        def f_exp(h):
+            nc.scalar.activation(out=p[h][:], in_=ns[h][:], func=ACT.Exp, scale=-1.0, bias=shift[h][:])
+
+        def f_pg(h):
+            nc.vector.tensor_reduce(out=pg[h][:, 0:HG], in_=runs(p[h][:]), axis=AX.X, op=ALU.add)
+
+        def f_rec(h):
+            width = HG + 1 - h
+            nc.vector.reciprocal(out=rpg[h][:, 0:width], in_=pg[h][:, 0:width])
+
+        def f_k(h):
+            stt(k[h][:], rpg[h][:, 0:HG], BIG, half(eg, h, HG), ALU.min, ALU.mult)
+
+        def f_w(h, g0, g1n):
+            s = slice(g0 * RUN, g1n * RUN)
+            tt(runs(w[h][:, s]), runs(p[h][:, s]), k[h][:, g0:g1n].unsqueeze(2).to_broadcast([P, g1n - g0, RUN]), ALU.mult)
+            nc.scalar.activation(out=th[h][:, s], in_=w[h][:, s], func=ACT.Tanh, scale=row_gain[:])
+
+        def f_out(h, g0, g1n):
+            s = slice(g0 * RUN, g1n * RUN)
+            so = slice(h * HS + g0 * RUN, h * HS + g1n * RUN)
+            tt(y[h][:, s], th[h][:, s], base_t[:, so], ALU.add)
+            nc.sync.dma_start(out=out[:, so], in_=y[h][:, s])
+
+        def cut(lst, h):
+            return a[:].indirect(half(lst, h, HS // 16))
 
         both = range(HALVES)
         for h in both:
@@ -126,53 +182,41 @@ def tile_attend_spreadof3_bestofruns_gated_heads_kernel(
         for h in both:
             nc.scalar.activation(out=g3[h][:], in_=cut(o3, h), func=ACT.Copy)
         for h in both:
-            nc.vector.tensor_tensor(out=z[h][:], in0=g1[h][:], in1=g2[h][:], op=ALU.subtract)
-        for h in both:
-            nc.vector.scalar_tensor_tensor(
-                out=mid[h][:], in0=z[h][:], scalar=0.5, in1=g2[h][:], op0=ALU.mult, op1=ALU.add
-            )
+            tt(z[h][:], g1[h][:], g2[h][:], ALU.subtract)
             nc.scalar.activation(out=az[h][:], in_=z[h][:], func=ACT.Abs, scale=0.5)
         for h in both:
-            nc.vector.tensor_tensor(out=c[h][:], in0=g3[h][:], in1=mid[h][:], op=ALU.subtract)
+            stt(mid[h][:], z[h][:], 0.5, g2[h][:], ALU.mult, ALU.add)
+        for h in both:
+            tt(c[h][:], g3[h][:], mid[h][:], ALU.subtract)
             nc.scalar.activation(out=ac[h][:], in_=c[h][:], func=ACT.Abs)
-        for h in both:
-            nc.vector.scalar_tensor_tensor(
-                out=mean[h][:], in0=c[h][:], scalar=1.0 / 3.0, in1=mid[h][:], op0=ALU.mult, op1=ALU.add
-            )
-        for h in both:
-            nc.vector.tensor_tensor(out=mx[h][:], in0=az[h][:], in1=ac[h][:], op=ALU.max)
-        for h in both:
-            nc.vector.tensor_tensor(out=spread[h][:], in0=mx[h][:], in1=az[h][:], op=ALU.add)
-        for h in both:
-            nc.vector.scalar_tensor_tensor(
-                out=ns[h][:], in0=spread[h][:], scalar=lam_t[:], in1=mean[h][:], op0=ALU.mult, op1=ALU.subtract
-            )
-        for h in both:
-            nc.vector.tensor_reduce(out=nbm[:, h * HG : (h + 1) * HG], in_=runs(ns[h][:]), axis=AX.X, op=ALU.min)
-        for h in both:
-            nc.vector.tensor_reduce(out=shift[h][:], in_=nbm[:, 0 : (h + 1) * HG], axis=AX.X, op=ALU.min)
-        for h in both:
-            nc.scalar.activation(out=p[h][:], in_=ns[h][:], func=ACT.Exp, scale=-1.0, bias=shift[h][:])
+        nc.scalar.activation(out=gain128[:], in_=gain_t[:], func=ACT.Copy, scale=128.0)
+        f_u(0)
+        f_u(1)
+        f_v(0)
+        f_mx(0)
+        f_v(1)
+        f_ns(0)
+        f_mx(1)
+        f_bm(0)
+        f_ns(1)
+        f_shift(0)
+        f_exp(0)
+        f_bm(1)
+        f_shift(1)
         nc.scalar.activation(
-            out=eg[:], in_=nbm[:], func=ACT.Exp, scale=-1.0, bias=shift[HALVES - 1][:], accum_out=eg_sum[:]
+            out=eg[:], in_=nbm[:], func=ACT.Exp, scale=-1.0, bias=shift[HALVES - 1][:], accum_out=pg[0][:, HG : HG + 1]
         )
-        for h in both:
-            nc.vector.tensor_reduce(out=pg[h][:], in_=runs(p[h][:]), axis=AX.X, op=ALU.add)
-        nc.vector.reciprocal(out=r_sum[:], in_=eg_sum[:])
-        for h in both:
-            nc.vector.reciprocal(out=rpg[h][:], in_=pg[h][:])
-        nc.vector.tensor_scalar(
-            out=row_gain[:], in0=r_sum[:], scalar1=gain_t[:], scalar2=128.0, op0=ALU.mult, op1=ALU.mult
-        )
-        for h in both:
-            nc.vector.scalar_tensor_tensor(
-                out=k[h][:], in0=rpg[h][:], scalar=BIG, in1=eg[:, h * HG : (h + 1) * HG], op0=ALU.min, op1=ALU.mult
-            )
-        for h in both:
-            nc.vector.tensor_tensor(
-                out=runs(w[h][:]), in0=runs(p[h][:]), in1=k[h][:].unsqueeze(2).to_broadcast([P, HG, RUN]), op=ALU.mult
-            )
-            nc.scalar.activation(out=th[h][:], in_=w[h][:], func=ACT.Tanh, scale=row_gain[:])
-        for h in both:
-            nc.vector.tensor_tensor(out=y[h][:], in0=th[h][:], in1=base_t[:, h * HS : (h + 1) * HS], op=ALU.add)
-            nc.sync.dma_start(out=out[:, h * HS : (h + 1) * HS], in_=y[h][:])
+        f_exp(1)
+        f_pg(0)
+        f_rec(0)
+        nc.scalar.activation(out=row_gain[:], in_=rpg[0][:, HG : HG + 1], func=ACT.Copy, scale=gain128[:])
+        f_pg(1)
+        f_k(0)
+        f_rec(1)
+        f_w(0, 0, HG)
+        f_k(1)
+        f_w(1, 0, HG // 2)
+        f_w(1, HG // 2, HG)
+        f_out(0, 0, HG)
+        f_out(1, 0, HG // 2)
+        f_out(1, HG // 2, HG)

@@ -49,15 +49,13 @@ def tile_attend_spreadof3_bestofruns_gated_heads_kernel(
                 out=k_words[u][:].bitcast(I32), in_=word_rows[:, u * 2 * T : (u + 1) * 2 * T].bitcast(I32)
             )
 
-        load_words(0)
-        k_planes = sb.tile([P, CW], U8, name="k_planes", align_bytes=64)
-        nc.vector.memset(k_planes[:].bitcast(I32), 0)
+        k_plane = sb.tile([P, T], U8, name="k_plane", align_bytes=64)
         scale_words = keys_scales[0].bitcast(I32)
         for quad in range(4):
             nc.sync.dma_start(
-                out=k_planes[32 * quad : 32 * quad + 16, :].bitcast(I32),
-                in_=scale_words[4 * quad : 4 * quad + 4, :].rearrange("r (j c) -> j r c", j=CHUNKS),
+                out=k_plane[32 * quad : 32 * quad + 4, :].bitcast(I32), in_=scale_words[4 * quad : 4 * quad + 4, :]
             )
+        load_words(0)
         load_words(1)
 
         o1 = lists.tile([P, I // 16], U16, name="o1")
@@ -89,13 +87,12 @@ def tile_attend_spreadof3_bestofruns_gated_heads_kernel(
             bank = ps.tile([P, width], F32, name=f"bank{n}")
             kw = k_words[t0 // (T // 2)]
             c0 = t0 % (T // 2)
-            j, s0 = divmod(t0, CW)
             nc.tensor.matmul_mx(
                 out=bank[:],
                 lhsT=q_words[:].bitcast(FP8X4),
                 lhsT_scale=q_plane[:],
                 rhs=kw[:, c0 : c0 + width].bitcast(FP8X4),
-                rhs_scale=k_planes[4 * j : P, s0 : s0 + width],
+                rhs_scale=k_plane[:, t0 : t0 + width],
                 start=True,
                 stop=True,
             )

@@ -38,6 +38,15 @@ def tile_attend_spreadof3_bestofruns_gated_heads_kernel(
         sb = ctx.enter_context(tc.tile_pool(name="sb", bufs=1))
         ps = ctx.enter_context(tc.psum_pool(name="ps", bufs=1))
 
+        k_plane = sb.tile([P, T], U8, name="k_plane", align_bytes=64)
+        scale_words = keys_scales[0].bitcast(I32)
+
+        def load_scales(queue, quad):
+            queue.dma_start(
+                out=k_plane[32 * quad : 32 * quad + 4, :].bitcast(I32), in_=scale_words[4 * quad : 4 * quad + 4, :]
+            )
+
+        load_scales(nc.scalar, 0)
         q_raw = sb.tile([P, PACK, Q], F32, name="q_raw")
         nc.sync.dma_start(out=q_raw[:], in_=query.rearrange("(p j) q -> p j q", j=PACK))
 
@@ -49,12 +58,8 @@ def tile_attend_spreadof3_bestofruns_gated_heads_kernel(
                 out=k_words[u][:].bitcast(I32), in_=word_rows[:, u * 2 * T : (u + 1) * 2 * T].bitcast(I32)
             )
 
-        k_plane = sb.tile([P, T], U8, name="k_plane", align_bytes=64)
-        scale_words = keys_scales[0].bitcast(I32)
-        for quad in range(4):
-            nc.sync.dma_start(
-                out=k_plane[32 * quad : 32 * quad + 4, :].bitcast(I32), in_=scale_words[4 * quad : 4 * quad + 4, :]
-            )
+        for quad in range(1, 4):
+            load_scales(nc.sync, quad)
         load_words(0)
         load_words(1)
 
@@ -115,7 +120,6 @@ def tile_attend_spreadof3_bestofruns_gated_heads_kernel(
         nbm = sb.tile([P, G], F32, name="nbm")
         eg = sb.tile([P, G], F32, name="eg")
         shift = halves("shift", 1)
-        gain128 = sb.tile([P, 1], F32, name="gain128")
         row_gain = sb.tile([P, 1], F32, name="row_gain")
 
         def runs(t):
@@ -160,7 +164,8 @@ def tile_attend_spreadof3_bestofruns_gated_heads_kernel(
 
         def f_w(h, g0, g1n):
             s = slice(g0 * RUN, g1n * RUN)
-            tt(runs(w[h][:, s]), runs(p[h][:, s]), k[h][:, g0:g1n].unsqueeze(2).to_broadcast([P, g1n - g0, RUN]), ALU.mult)
+            spread = k[h][:, g0:g1n].unsqueeze(2).to_broadcast([P, g1n - g0, RUN])
+            stt(runs(w[h][:, s]), runs(p[h][:, s]), 128.0, spread, ALU.mult, ALU.mult)
             nc.scalar.activation(out=th[h][:, s], in_=w[h][:, s], func=ACT.Tanh, scale=row_gain[:])
 
         def f_out(h, g0, g1n):
@@ -186,7 +191,6 @@ def tile_attend_spreadof3_bestofruns_gated_heads_kernel(
         for h in both:
             tt(c[h][:], g3[h][:], mid[h][:], ALU.subtract)
             nc.scalar.activation(out=ac[h][:], in_=c[h][:], func=ACT.Abs)
-        nc.scalar.activation(out=gain128[:], in_=gain_t[:], func=ACT.Copy, scale=128.0)
         f_u(0)
         f_u(1)
         f_v(0)
@@ -206,7 +210,7 @@ def tile_attend_spreadof3_bestofruns_gated_heads_kernel(
         f_exp(1)
         f_pg(0)
         f_rec(0)
-        nc.scalar.activation(out=row_gain[:], in_=rpg[0][:, HG : HG + 1], func=ACT.Copy, scale=gain128[:])
+        nc.scalar.activation(out=row_gain[:], in_=rpg[0][:, HG : HG + 1], func=ACT.Copy, scale=gain_t[:])
         f_pg(1)
         f_k(0)
         f_rec(1)

from contextlib import ExitStack

import concourse.mybir as mybir

D, T, I, Q, G = 512, 1024, 512, 128, 64
RUN = I // G
FLOPS = 2 * D * T * Q

F32 = mybir.dt.float32
BF16 = mybir.dt.bfloat16
I32 = mybir.dt.int32
U32 = mybir.dt.uint32
U16 = mybir.dt.uint16
U8 = mybir.dt.uint8
FP8X4 = mybir.dt.float8_e4m3fn_x4
ALU = mybir.AluOpType
ACT = mybir.ActivationFunctionType
AX = mybir.AxisListType

P = 128
PACK = 4
CHUNKS = 4
CW = T // CHUNKS
HALVES = 2
HS = I // HALVES
HG = G // HALVES
BIG = 3.0e38
QV = 22
PASSES = ((0, 256), (256, 256), (512, 256), (768, 128), (896, 128))


def tile_attend_spreadof3_bestofruns_gated_heads_kernel(
    tc, query, keys_words, keys_scales, lam, base, gain2, offs, offs2, offs3, out
):
    nc = tc.nc
    with ExitStack() as ctx:
        lists = ctx.enter_context(tc.tile_pool(name="lists", bufs=1))
        sb = ctx.enter_context(tc.tile_pool(name="sb", bufs=1))
        ps = ctx.enter_context(tc.psum_pool(name="ps", bufs=1))

        k_plane = sb.tile([P, T], U8, name="k_plane", align_bytes=64)
        scale_words = keys_scales[0].bitcast(I32)

        def load_scales(queue, quad):
            queue.dma_start(
                out=k_plane[32 * quad : 32 * quad + 4, :].bitcast(I32), in_=scale_words[4 * quad : 4 * quad + 4, :]
            )

        load_scales(nc.scalar, 0)
        q_raw = sb.tile([P, PACK, Q], F32, name="q_raw")
        nc.sync.dma_start(out=q_raw[:], in_=query.rearrange("(p j) q -> p j q", j=PACK))

        word_rows = keys_words[0].rearrange("p n t -> p (n t)")
        k_words = [sb.tile([P, T // 2], U32, name=f"k_words{u}", align_bytes=64) for u in range(2)]

        def load_words(u):
            nc.sync.dma_start(
                out=k_words[u][:].bitcast(I32), in_=word_rows[:, u * 2 * T : (u + 1) * 2 * T].bitcast(I32)
            )

        for quad in range(1, 4):
            load_scales(nc.sync, quad)
        load_words(0)
        load_words(1)

        o1 = lists.tile([P, I // 16], U16, name="o1")
        o2 = lists.tile([P, I // 16], U16, name="o2")
        o3 = lists.tile([P, I // 16], U16, name="o3")
        nc.sync.dma_start(o2[:], offs2)
        nc.sync.dma_start(o1[:], offs)
        nc.sync.dma_start(o3[:], offs3)
        lam_t = sb.tile([P, 1], F32, name="lam_t")
        gain_t = sb.tile([P, 1], F32, name="gain_t")
        base_t = sb.tile([P, I], F32, name="base_t")
        nc.sync.dma_start(out=lam_t[:], in_=lam)
        nc.sync.dma_start(out=gain_t[:], in_=gain2)
        nc.sync.dma_start(out=base_t[:], in_=base)

        q_bf = sb.tile([P, Q, PACK], BF16, name="q_bf", align_bytes=64)
        q_dst = q_bf[:].rearrange("p (c i) t -> p c t i", i=4)
        q_src = q_raw[:].rearrange("p t (c i) -> p c t i", i=4)
        nc.vector.tensor_copy(out=q_dst[:, 0:QV], in_=q_src[:, 0:QV])
        nc.scalar.copy(out=q_dst[:, QV : Q // 4], in_=q_src[:, QV : Q // 4])
        q_words = sb.tile([P, Q], U32, name="q_words", align_bytes=64)
        q_plane = sb.tile([P, Q], U8, name="q_plane", align_bytes=64)
        nc.vector.quantize_mx(
            out=q_words[:].bitcast(FP8X4), scales=q_plane[:], in_=q_bf[:].rearrange("p q t -> p (q t)")
        )

        a = sb.tile([P, T], F32, name="a")
        for n, (t0, width) in enumerate(PASSES):
            bank = ps.tile([P, width], F32, name=f"bank{n}")
            kw = k_words[t0 // (T // 2)]
            c0 = t0 % (T // 2)
            nc.tensor.matmul_mx(
                out=bank[:],
                lhsT=q_words[:].bitcast(FP8X4),
                lhsT_scale=q_plane[:],
                rhs=kw[:, c0 : c0 + width].bitcast(FP8X4),
                rhs_scale=k_plane[:, t0 : t0 + width],
                start=True,
                stop=True,
            )
            if n % 2 == 1:
                nc.vector.tensor_copy(out=a[:, t0 : t0 + width], in_=bank[:])
            else:
                nc.scalar.activation(out=a[:, t0 : t0 + width], in_=bank[:], func=ACT.Copy)

        def halves(name, width=HS):
            return [sb.tile([P, width], F32, name=f"{name}{h}") for h in range(HALVES)]

        def half(t, h, width=HS):
            return t[:, h * width : (h + 1) * width]

        g1, g2, g3 = halves("g1"), halves("g2"), halves("g3")
        z, mid, c, u, v = halves("z"), halves("mid"), halves("c"), halves("u"), halves("v")
        az, ac, mx, ns = halves("az"), halves("ac"), halves("mx"), halves("ns")
        p, w, th, y = halves("p"), halves("w"), halves("th"), halves("y")
        pg, rpg, k = halves("pg", HG + 1), halves("rpg", HG + 1), halves("k", HG)
        nbm = sb.tile([P, G], F32, name="nbm")
        eg = sb.tile([P, G], F32, name="eg")
        shift = halves("shift", 1)
        row_gain = sb.tile([P, 1], F32, name="row_gain")

        def runs(t):
            return t.rearrange("p (g e) -> p g e", e=RUN)

        def tt(o, i0, i1, op):
            nc.vector.tensor_tensor(out=o, in0=i0, in1=i1, op=op)

        def stt(o, i0, s, i1, op0, op1):
            nc.vector.scalar_tensor_tensor(out=o, in0=i0, scalar=s, in1=i1, op0=op0, op1=op1)

        def f_u(h):
            stt(u[h][:], az[h][:], lam_t[:], mid[h][:], ALU.mult, ALU.subtract)

        def f_v(h):
            stt(v[h][:], c[h][:], -1.0 / 3.0, u[h][:], ALU.mult, ALU.add)

        def f_mx(h):
            tt(mx[h][:], az[h][:], ac[h][:], ALU.max)

        def f_ns(h):
            stt(ns[h][:], mx[h][:], lam_t[:], v[h][:], ALU.mult, ALU.add)

        def f_bm(h):
            nc.vector.tensor_reduce(out=half(nbm, h, HG), in_=runs(ns[h][:]), axis=AX.X, op=ALU.min)

        def f_shift(h):
            nc.vector.tensor_reduce(out=shift[h][:], in_=nbm[:, 0 : (h + 1) * HG], axis=AX.X, op=ALU.min)

        def f_exp(h):
            nc.scalar.activation(out=p[h][:], in_=ns[h][:], func=ACT.Exp, scale=-1.0, bias=shift[h][:])

        def f_pg(h):
            nc.vector.tensor_reduce(out=pg[h][:, 0:HG], in_=runs(p[h][:]), axis=AX.X, op=ALU.add)

        def f_rec(h):
            width = HG + 1 - h
            nc.vector.reciprocal(out=rpg[h][:, 0:width], in_=pg[h][:, 0:width])

        def f_k(h):
            stt(k[h][:], rpg[h][:, 0:HG], BIG, half(eg, h, HG), ALU.min, ALU.mult)

        def f_w(h, g0, g1n):
            s = slice(g0 * RUN, g1n * RUN)
            spread = k[h][:, g0:g1n].unsqueeze(2).to_broadcast([P, g1n - g0, RUN])
            stt(runs(w[h][:, s]), runs(p[h][:, s]), 128.0, spread, ALU.mult, ALU.mult)
            nc.scalar.activation(out=th[h][:, s], in_=w[h][:, s], func=ACT.Tanh, scale=row_gain[:])

        def f_out(h, g0, g1n):
            s = slice(g0 * RUN, g1n * RUN)
            so = slice(h * HS + g0 * RUN, h * HS + g1n * RUN)
            tt(y[h][:, s], th[h][:, s], base_t[:, so], ALU.add)
            nc.sync.dma_start(out=out[:, so], in_=y[h][:, s])

        def cut(lst, h):
            return a[:].indirect(half(lst, h, HS // 16))

        both = range(HALVES)
        for h in both:
            nc.vector.tensor_copy(out=g1[h][:], in_=cut(o1, h))
            nc.scalar.activation(out=g2[h][:], in_=cut(o2, h), func=ACT.Copy)
        for h in both:
            nc.scalar.activation(out=g3[h][:], in_=cut(o3, h), func=ACT.Copy)
        for h in both:
            tt(z[h][:], g1[h][:], g2[h][:], ALU.subtract)
            nc.scalar.activation(out=az[h][:], in_=z[h][:], func=ACT.Abs, scale=0.5)
        for h in both:
            stt(mid[h][:], z[h][:], 0.5, g2[h][:], ALU.mult, ALU.add)
        for h in both:
            tt(c[h][:], g3[h][:], mid[h][:], ALU.subtract)
            nc.scalar.activation(out=ac[h][:], in_=c[h][:], func=ACT.Abs)
        f_u(0)
        f_u(1)
        f_v(0)
        f_mx(0)
        f_v(1)
        f_ns(0)
        f_mx(1)
        f_bm(0)
        f_ns(1)
        f_shift(0)
        f_exp(0)
        f_bm(1)
        f_shift(1)
        nc.scalar.activation(
            out=eg[:], in_=nbm[:], func=ACT.Exp, scale=-1.0, bias=shift[HALVES - 1][:], accum_out=pg[0][:, HG : HG + 1]
        )
        f_exp(1)
        f_pg(0)
        f_rec(0)
        nc.scalar.activation(out=row_gain[:], in_=rpg[0][:, HG : HG + 1], func=ACT.Copy, scale=gain_t[:])
        f_pg(1)
        f_k(0)
        f_rec(1)
        f_w(0, 0, HG)
        f_k(1)
        f_w(1, 0, HG // 2)
        f_w(1, HG // 2, HG)
        f_out(0, 0, HG)
        f_out(1, 0, HG // 2)
        f_out(1, HG // 2, HG)
